import numpy as np
import ml_dtypes


def mxq(x, axis, fmt="e4m3"):
    dtype, down = {"e4m3": (ml_dtypes.float8_e4m3fn, 7), "e5m2": (ml_dtypes.float8_e5m2, 14)}[fmt]
    v = np.moveaxis(np.asarray(x, np.float32).astype(ml_dtypes.bfloat16).astype(np.float64), axis, -1)
    blocks = v.reshape(v.shape[:-1] + (-1, 32))
    amax = np.abs(blocks).max(-1, keepdims=True)
    byte = np.maximum(np.where(amax > 0, np.frexp(amax)[1] - 1 + 127, 0) - down, 1)
    scale = np.exp2(byte - 127.0)
    codes = (blocks / scale).astype(np.float32).astype(dtype).astype(np.float64)
    return np.moveaxis((codes * scale).reshape(v.shape), -1, axis)


WIDE = False


def mx_kscale(k):
    if not WIDE:
        return np.ones(k)
    levels = np.array([10, -10, 5, -5, 0])
    if k % 512:
        return np.exp2(np.random.permutation(np.resize(levels, k // 32))).repeat(32)
    a = np.empty((k // 512, 16))
    for p in range(k // 512):
        a[p, :8] = np.random.permutation(np.resize(levels, 8))
        for g in range(8):
            far = levels[np.abs(levels - a[p, g]) >= 10]
            a[p, g + 8] = far[np.random.randint(len(far))]
    return np.exp2(a.ravel()).repeat(32)


def f64(x):
    return np.asarray(x).astype(np.float64)


def striped(idx):
    return np.tile(idx.reshape(-1, 16).T, (8, 1)).astype(np.uint16)


def unstriped(offs):
    return offs[:16].T.reshape(-1).astype(np.int64)


def pack_weight(w):
    k, n = w.shape
    w = f64(np.asarray(w, np.float32).astype(ml_dtypes.bfloat16)).reshape(k // 32, 32, n)
    amax = np.abs(w).max(1)
    byte = np.clip(np.where(amax > 0, np.frexp(amax)[1] - 1 + 127 - 7, 1), 1, 254)
    scaled = (w * np.exp2(127.0 - byte)[:, None, :]).reshape(k, n).astype(np.float32)
    words = np.ascontiguousarray(scaled.reshape(k // 512, 128, 4, n).transpose(0, 1, 3, 2)).astype(ml_dtypes.float8_e4m3fn).view(np.uint8)
    return words, np.ascontiguousarray(byte.astype(np.uint8).reshape(k // 512, 16, n))


def unpack_weight(words, scales):
    g, p, n, _ = words.shape
    vals = np.ascontiguousarray(words).view(ml_dtypes.float8_e4m3fn).astype(np.float64) * np.repeat(np.exp2(scales.astype(np.float64) - 127.0), 8, axis=1)[..., None]
    return vals.transpose(0, 1, 3, 2).reshape(g * 512, n)


def sigmoid(v):
    return 1.0 / (1.0 + np.exp(-np.maximum(v, -700.0)))


K, T, S, D, N, H, V, W = 512, 2048, 512, 4, 256, 512, 128, 2048


def setup_inputs():
    n = np.random.standard_normal
    s = mx_kscale(K)[:, None]
    u = mx_kscale(H)
    packed_xT = pack_weight(n((K, T)) * s)
    packed_eT = pack_weight(n((K, W)) * s)
    return {
        "x_words": packed_xT[0],
        "x_scales": packed_xT[1],
        "w1": (n((K, H)) / np.sqrt(K) / s).astype(np.float32),
        "e_words": packed_eT[0],
        "e_scales": packed_eT[1],
        "w2": (n((K, H)) / np.sqrt(K) / s).astype(np.float32),
        "lab": (np.random.uniform(0.0, 1.0, (H, V))).astype(np.float32),
        "unit": (np.random.uniform(0.6, 1.4, (H, 1)) * u[:, None]).astype(np.float32),
        "w3": (n((H, N)) / np.sqrt(H) / u[:, None]).astype(np.float32),
        "offs": striped(np.random.permutation(T)[:S]),
        "rstp": striped(np.random.permutation(W)[:S]),
    }


def reference(x_words, x_scales, w1, e_words, e_scales, w2, lab, unit, w3, offs, rstp):
    xq = unpack_weight(x_words, x_scales)[:, unstriped(offs)]
    y = mxq(f64(w1), 0, "e4m3").T @ xq
    e_rstp = unpack_weight(e_words, e_scales)[:, unstriped(rstp)]
    ye = mxq(f64(w2), 0, "e4m3").T @ e_rstp
    imp = 0.8 * np.tanh(y - ye)
    tot = imp.reshape(len(imp), -1, D).sum(axis=2)
    acc = sigmoid(tot)
    err = acc - f64(lab)
    two = imp + np.pad(imp, ((0, 0), (0, 1)))[:, 1:]
    ec = np.repeat(err, D, axis=1) * two
    hid = f64(unit) * ec
    return mxq(f64(w3), 0, "e4m3").T @ mxq(hid, 0, "e4m3")

@@ -1,0 +1,265 @@
+from contextlib import ExitStack
+
+import concourse.mybir as mybir
+
+K, T, S, D, N, H = 512, 2048, 512, 4, 256, 512
+V = S // D
+P = 128
+PACK = 4
+CH = 128
+NCH = S // CH
+HALF = S // 2
+SPLIT = 44
+FLOPS = 2 * (2 * K * H * S + H * N * S)
+
+F32 = mybir.dt.float32
+BF16 = mybir.dt.bfloat16
+I32 = mybir.dt.int32
+U32 = mybir.dt.uint32
+U16 = mybir.dt.uint16
+U8 = mybir.dt.uint8
+FP8X4 = mybir.dt.float8_e4m3fn_x4
+ALU = mybir.AluOpType
+ACT = mybir.ActivationFunctionType
+
+
+def tile_picked_yprimr_step_p_kernel(
+    tc, x_words, x_scales, w1, e_words, e_scales, w2, lab, unit, w3, offs, rstp, out
+):
+    nc = tc.nc
+    with ExitStack() as ctx:
+        sb = ctx.enter_context(tc.tile_pool(name="sb", bufs=1))
+        ps = ctx.enter_context(tc.psum_pool(name="ps", bufs=1))
+
+        def tile(name, shape, dtype):
+            return sb.tile(shape, dtype, name=name, align_bytes=64)
+
+        offs_t = tile("offs_t", [P, S // 16], U16)
+        rstp_t = tile("rstp_t", [P, S // 16], U16)
+        xw = tile("xw", [P, T], U32)
+        ew = tile("ew", [P, T], U32)
+        xs = tile("xs", [P, T], U8)
+        es = tile("es", [P, T], U8)
+        w1_raw = tile("w1_raw", [P, PACK * H], F32)
+        w2_raw = tile("w2_raw", [P, PACK * H], F32)
+        w3_raw = tile("w3_raw", [P, PACK * N], F32)
+        lab_t = tile("lab_t", [P, PACK * V], F32)
+        unit_t = tile("unit_t", [P, PACK], F32)
+        th = tile("th", [P, (S + 1) * PACK], F32)
+
+        nc.vector.memset(xs[:].bitcast(U32), 0)
+        nc.vector.memset(es[:].bitcast(U32), 0)
+        nc.vector.memset(th[:, S * PACK :], 0.0)
+
+        def load_scale_rows(plane, rows, q):
+            nc.sync.dma_start(
+                out=plane[32 * q : 32 * q + 4, :].bitcast(I32),
+                in_=rows[0, 4 * q : 4 * q + 4, :].bitcast(I32),
+            )
+
+        def load_words(window, words):
+            nc.sync.dma_start(
+                out=window[:].bitcast(I32),
+                in_=words[0].rearrange("p n t -> p (n t)").bitcast(I32),
+            )
+
+        def load_rows(dst, src):
+            nc.sync.dma_start(out=dst[:], in_=src.rearrange("(p j) c -> p (j c)", j=PACK))
+
+        load_rows(w1_raw, w1)
+        for q in range(4):
+            load_scale_rows(xs, x_scales, q)
+        nc.sync.dma_start(offs_t[:], offs)
+        load_words(xw, x_words)
+        for q in range(4):
+            load_scale_rows(es, e_scales, q)
+        nc.sync.dma_start(rstp_t[:], rstp)
+        load_rows(w2_raw, w2)
+        load_words(ew, e_words)
+        load_rows(unit_t, unit)
+        load_rows(lab_t, lab)
+        load_rows(w3_raw, w3)
+
+        xg_s = tile("xg_s", [P, S], U8)
+        eg_s = tile("eg_s", [P, S], U8)
+        xg_w = tile("xg_w", [P, S], U32)
+        eg_w = [tile("eg_w%d" % h, [P, HALF], U32) for h in range(2)]
+        w1_bf = tile("w1_bf", [P, H * PACK], BF16)
+        w2_bf = tile("w2_bf", [P, H * PACK], BF16)
+        w3_bf = tile("w3_bf", [P, N * PACK], BF16)
+        w1_c = tile("w1_c", [P, H], U32)
+        w2_c = tile("w2_c", [P, H], U32)
+        w3_c = tile("w3_c", [P, N], U32)
+        w1_s = tile("w1_s", [P, H], U8)
+        w2_s = tile("w2_s", [P, H], U8)
+        w3_s = tile("w3_s", [P, N], U8)
+
+        def dealt_in(raw):
+            return raw[:].rearrange("p (j m t) -> p m j t", j=PACK, t=PACK)
+
+        def dealt_out(bf):
+            return bf[:].rearrange("p (t m j) -> p m j t", t=PACK, j=PACK)
+
+        nc.vector.tensor_copy(xg_s[:], xs[:].indirect(offs_t[:]))
+        def round_and_deal(bf, raw, sign):
+            nc.scalar.activation(dealt_out(bf)[:, :SPLIT], dealt_in(raw)[:, :SPLIT], ACT.Copy, scale=sign)
+            nc.vector.tensor_scalar(
+                dealt_out(bf)[:, SPLIT:], dealt_in(raw)[:, SPLIT:], sign, None, ALU.mult
+            )
+
+        round_and_deal(w1_bf, w1_raw, 1.0)
+        nc.vector.quantize_mx(out=w1_c[:].bitcast(FP8X4), scales=w1_s[:], in_=w1_bf[:])
+        nc.vector.tensor_copy(xg_w[:], xw[:].indirect(offs_t[:]))
+        nc.vector.tensor_copy(eg_s[:], es[:].indirect(rstp_t[:]))
+        round_and_deal(w2_bf, w2_raw, -1.0)
+        nc.vector.quantize_mx(out=w2_c[:].bitcast(FP8X4), scales=w2_s[:], in_=w2_bf[:])
+
+        diff = [ps.tile([P, PACK * CH], F32, name="diff%d" % c) for c in range(NCH)]
+        for c in range(NCH):
+            cols = slice(c * CH, (c + 1) * CH)
+            for t in range(PACK):
+                m = slice(t * P, (t + 1) * P)
+                nc.tensor.matmul_mx(
+                    out=diff[c][:, t * CH : (t + 1) * CH],
+                    lhsT=w1_c[:, m].bitcast(FP8X4), lhsT_scale=w1_s[:, m],
+                    rhs=xg_w[:, cols].bitcast(FP8X4), rhs_scale=xg_s[:, cols],
+                    start=(t == 0), stop=False,
+                )
+
+        for h in range(2):
+            nc.vector.tensor_copy(eg_w[h][:], ew[:].indirect(rstp_t[:, h * HALF // 16 : (h + 1) * HALF // 16]))
+
+        for c in range(NCH):
+            cols = slice(c * CH, (c + 1) * CH)
+            local = slice((c % 2) * CH, (c % 2 + 1) * CH)
+            for t in range(PACK):
+                m = slice(t * P, (t + 1) * P)
+                nc.tensor.matmul_mx(
+                    out=diff[c][:, t * CH : (t + 1) * CH],
+                    lhsT=w2_c[:, m].bitcast(FP8X4), lhsT_scale=w2_s[:, m],
+                    rhs=eg_w[c // 2][:, local].bitcast(FP8X4), rhs_scale=eg_s[:, cols],
+                    start=False, stop=(t == PACK - 1),
+                )
+
+        two = tile("two", [P, S * PACK], F32)
+        tot = tile("tot", [P, V * PACK], F32)
+        half_tanh = tile("half_tanh", [P, V * PACK], F32)
+        dev = tile("dev", [P, V * PACK], F32)
+        coef = tile("coef", [P, V * PACK], F32)
+        unit4 = tile("unit4", [P, PACK], F32)
+        hid = [tile("hid%d" % c, [P, CH * PACK], BF16) for c in range(NCH)]
+        hid_c = [tile("hid_c%d" % c, [P, CH], U32) for c in range(NCH)]
+        hid_s = [tile("hid_s%d" % c, [P, CH], U8) for c in range(NCH)]
+        res = [tile("res%d" % c, [P, 2 * CH], F32) for c in range(NCH)]
+        acc = [ps.tile([P, 2 * CH], F32, name="acc%d" % c) for c in range(NCH)]
+        VH = V // 2
+
+        def do_tanh(c):
+            nc.scalar.activation(
+                th[:, c * CH * PACK : (c + 1) * CH * PACK].rearrange("p (j t) -> p j t", t=PACK),
+                diff[c][:].rearrange("p (t j) -> p j t", t=PACK),
+                ACT.Tanh,
+            )
+
+        def do_two(c):
+            lo = max(c * CH - 1, 0)
+            hi = S if c == NCH - 1 else (c + 1) * CH - 1
+            nc.vector.tensor_tensor(
+                two[:, lo * PACK : hi * PACK], th[:, lo * PACK : hi * PACK],
+                th[:, (lo + 1) * PACK : (hi + 1) * PACK], ALU.add,
+            )
+
+        def vslice(h):
+            return slice(h * VH * PACK, (h + 1) * VH * PACK)
+
+        def do_tot(h):
+            g = two[:, h * HALF * PACK : (h + 1) * HALF * PACK].rearrange("p (v d t) -> p v d t", d=D, t=PACK)
+            nc.vector.tensor_tensor(
+                tot[:, vslice(h)].rearrange("p (v t) -> p v t", t=PACK), g[:, :, 0, :], g[:, :, 2, :], ALU.add
+            )
+
+        def do_sig(h):
+            nc.scalar.activation(half_tanh[:, vslice(h)], tot[:, vslice(h)], ACT.Tanh, scale=0.4)
+
+        def do_dev(h):
+            nc.vector.scalar_tensor_tensor(
+                dev[:, vslice(h)].rearrange("p (v t) -> p v t", t=PACK),
+                lab_t[:].rearrange("p (t v) -> p v t", t=PACK)[:, h * VH : (h + 1) * VH, :],
+                -2.0,
+                half_tanh[:, vslice(h)].rearrange("p (v t) -> p v t", t=PACK),
+                ALU.mult, ALU.add,
+            )
+
+        def do_coef(h):
+            nc.vector.scalar_tensor_tensor(
+                coef[:, vslice(h)].rearrange("p (v t) -> p v t", t=PACK),
+                dev[:, vslice(h)].rearrange("p (v t) -> p v t", t=PACK),
+                1.0,
+                unit4[:].unsqueeze(1).to_broadcast([P, VH, PACK]),
+                ALU.add, ALU.mult,
+            )
+
+        def do_hid(c):
+            vc = CH // D
+            nc.vector.tensor_tensor(
+                hid[c][:].rearrange("p (v d t) -> p v d t", d=D, t=PACK),
+                two[:, c * CH * PACK : (c + 1) * CH * PACK].rearrange("p (v d t) -> p v d t", d=D, t=PACK),
+                coef[:, c * vc * PACK : (c + 1) * vc * PACK]
+                .rearrange("p (v t) -> p v t", t=PACK)
+                .unsqueeze(2)
+                .to_broadcast([P, vc, D, PACK]),
+                ALU.mult,
+            )
+
+        def do_quant(c):
+            nc.vector.quantize_mx(out=hid_c[c][:].bitcast(FP8X4), scales=hid_s[c][:], in_=hid[c][:])
+
+        def do_out(c):
+            for a in range(2):
+                m = slice(a * P, (a + 1) * P)
+                nc.tensor.matmul_mx(
+                    out=acc[c][:, a * CH : (a + 1) * CH],
+                    lhsT=w3_c[:, m].bitcast(FP8X4), lhsT_scale=w3_s[:, m],
+                    rhs=hid_c[c][:].bitcast(FP8X4), rhs_scale=hid_s[c][:],
+                    start=True, stop=True,
+                )
+            nc.scalar.copy(res[c][:], acc[c][:])
+            nc.sync.dma_start(
+                out=out[:, c * CH : (c + 1) * CH].rearrange("(a p) j -> p a j", a=2),
+                in_=res[c][:].rearrange("p (a j) -> p a j", a=2),
+            )
+
+        nc.scalar.activation(unit4[:], unit_t[:], ACT.Copy, scale=0.4)
+        do_tanh(0)
+        do_tanh(1)
+        do_two(0)
+        do_tanh(2)
+        do_two(1)
+        do_tanh(3)
+        do_two(2)
+        do_tot(0)
+        do_sig(0)
+        do_two(3)
+        do_dev(0)
+        do_tot(1)
+        do_sig(1)
+        nc.scalar.copy(
+            w3_bf[:].rearrange("p (c i j) -> p c j i", i=4, j=PACK),
+            w3_raw[:].rearrange("p (j c i) -> p c j i", i=4, j=PACK),
+        )
+        do_coef(0)
+        do_dev(1)
+        do_hid(0)
+        do_coef(1)
+        do_hid(1)
+        nc.vector.quantize_mx(out=w3_c[:].bitcast(FP8X4), scales=w3_s[:], in_=w3_bf[:])
+        do_quant(0)
+        do_hid(2)
+        do_out(0)
+        do_quant(1)
+        do_hid(3)
+        do_out(1)
+        do_quant(2)
+        do_quant(3)
+        do_out(2)
+        do_out(3)

@@ -9,7 +9,10 @@ PACK = 4
 CH = 128
 NCH = S // CH
 HALF = S // 2
-SPLIT = 44
+SPLIT1 = 44
+SPLIT2 = 44
+X_ROW = 4
+E_ROW = 8
 FLOPS = 2 * (2 * K * H * S + H * N * S)
 
 F32 = mybir.dt.float32
@@ -51,10 +54,10 @@ def tile_picked_yprimr_step_p_kernel(
         nc.vector.memset(es[:].bitcast(U32), 0)
         nc.vector.memset(th[:, S * PACK :], 0.0)
 
-        def load_scale_rows(plane, rows, q):
-            nc.sync.dma_start(
-                out=plane[32 * q : 32 * q + 4, :].bitcast(I32),
-                in_=rows[0, 4 * q : 4 * q + 4, :].bitcast(I32),
+        def load_scale_rows(queue, plane, rows, r, first):
+            queue.dma_start(
+                out=plane[first + r : P : 32, :].bitcast(I32),
+                in_=rows[0, r:16:4, :].bitcast(I32),
             )
 
         def load_words(window, words):
@@ -67,14 +70,14 @@ def tile_picked_yprimr_step_p_kernel(
             nc.sync.dma_start(out=dst[:], in_=src.rearrange("(p j) c -> p (j c)", j=PACK))
 
         load_rows(w1_raw, w1)
-        for q in range(4):
-            load_scale_rows(xs, x_scales, q)
+        for r in range(4):
+            load_scale_rows(nc.sync, xs, x_scales, r, X_ROW)
         nc.sync.dma_start(offs_t[:], offs)
-        load_words(xw, x_words)
-        for q in range(4):
-            load_scale_rows(es, e_scales, q)
-        nc.sync.dma_start(rstp_t[:], rstp)
         load_rows(w2_raw, w2)
+        for r in range(4):
+            load_scale_rows(nc.sync, es, e_scales, r, E_ROW)
+        nc.sync.dma_start(rstp_t[:], rstp)
+        load_words(xw, x_words)
         load_words(ew, e_words)
         load_rows(unit_t, unit)
         load_rows(lab_t, lab)
@@ -82,7 +85,7 @@ def tile_picked_yprimr_step_p_kernel(
 
         xg_s = tile("xg_s", [P, S], U8)
         eg_s = tile("eg_s", [P, S], U8)
-        xg_w = tile("xg_w", [P, S], U32)
+        xg_w = [tile("xg_w%d" % h, [P, HALF], U32) for h in range(2)]
         eg_w = [tile("eg_w%d" % h, [P, HALF], U32) for h in range(2)]
         w1_bf = tile("w1_bf", [P, H * PACK], BF16)
         w2_bf = tile("w2_bf", [P, H * PACK], BF16)
@@ -100,58 +103,61 @@ def tile_picked_yprimr_step_p_kernel(
         def dealt_out(bf):
             return bf[:].rearrange("p (t m j) -> p m j t", t=PACK, j=PACK)
 
-        nc.vector.tensor_copy(xg_s[:], xs[:].indirect(offs_t[:]))
-        def round_and_deal(bf, raw, sign):
-            nc.scalar.activation(dealt_out(bf)[:, :SPLIT], dealt_in(raw)[:, :SPLIT], ACT.Copy, scale=sign)
+        def round_and_deal(bf, raw, sign, split):
+            nc.scalar.activation(dealt_out(bf)[:, :split], dealt_in(raw)[:, :split], ACT.Copy, scale=sign)
             nc.vector.tensor_scalar(
-                dealt_out(bf)[:, SPLIT:], dealt_in(raw)[:, SPLIT:], sign, None, ALU.mult
+                dealt_out(bf)[:, split:], dealt_in(raw)[:, split:], sign, None, ALU.mult
             )
 
-        round_and_deal(w1_bf, w1_raw, 1.0)
+        round_and_deal(w1_bf, w1_raw, 1.0, SPLIT1)
+        nc.vector.tensor_copy(xg_s[:], xs[:].indirect(offs_t[:]))
         nc.vector.quantize_mx(out=w1_c[:].bitcast(FP8X4), scales=w1_s[:], in_=w1_bf[:])
-        nc.vector.tensor_copy(xg_w[:], xw[:].indirect(offs_t[:]))
+        round_and_deal(w2_bf, w2_raw, -1.0, SPLIT2)
         nc.vector.tensor_copy(eg_s[:], es[:].indirect(rstp_t[:]))
-        round_and_deal(w2_bf, w2_raw, -1.0)
         nc.vector.quantize_mx(out=w2_c[:].bitcast(FP8X4), scales=w2_s[:], in_=w2_bf[:])
 
-        diff = [ps.tile([P, PACK * CH], F32, name="diff%d" % c) for c in range(NCH)]
-        for c in range(NCH):
-            cols = slice(c * CH, (c + 1) * CH)
-            for t in range(PACK):
-                m = slice(t * P, (t + 1) * P)
-                nc.tensor.matmul_mx(
-                    out=diff[c][:, t * CH : (t + 1) * CH],
-                    lhsT=w1_c[:, m].bitcast(FP8X4), lhsT_scale=w1_s[:, m],
-                    rhs=xg_w[:, cols].bitcast(FP8X4), rhs_scale=xg_s[:, cols],
-                    start=(t == 0), stop=False,
+        def gather_words(picked, window, places):
+            for h in range(2):
+                nc.vector.tensor_copy(
+                    picked[h][:], window[:].indirect(places[:, h * HALF // 16 : (h + 1) * HALF // 16])
                 )
 
-        for h in range(2):
-            nc.vector.tensor_copy(eg_w[h][:], ew[:].indirect(rstp_t[:, h * HALF // 16 : (h + 1) * HALF // 16]))
+        diff = [ps.tile([P, PACK * CH], F32, name="diff%d" % c, tag="bank%d" % c) for c in range(NCH)]
 
-        for c in range(NCH):
+        def first_product(c, w_c, w_s, picked, picked_s, row, opens):
             cols = slice(c * CH, (c + 1) * CH)
             local = slice((c % 2) * CH, (c % 2 + 1) * CH)
             for t in range(PACK):
                 m = slice(t * P, (t + 1) * P)
                 nc.tensor.matmul_mx(
                     out=diff[c][:, t * CH : (t + 1) * CH],
-                    lhsT=w2_c[:, m].bitcast(FP8X4), lhsT_scale=w2_s[:, m],
-                    rhs=eg_w[c // 2][:, local].bitcast(FP8X4), rhs_scale=eg_s[:, cols],
-                    start=False, stop=(t == PACK - 1),
+                    lhsT=w_c[:, m].bitcast(FP8X4), lhsT_scale=w_s[:, m],
+                    rhs=picked[c // 2][:, local].bitcast(FP8X4), rhs_scale=picked_s[row:, cols],
+                    start=(opens and t == 0), stop=(not opens and t == PACK - 1),
                 )
+
+        gather_words(xg_w, xw, offs_t)
+        for c in range(2):
+            first_product(c, w1_c, w1_s, xg_w, xg_s, X_ROW, True)
+        gather_words(eg_w, ew, rstp_t)
+        for c in range(2):
+            first_product(c, w2_c, w2_s, eg_w, eg_s, E_ROW, False)
+        for c in range(2, NCH):
+            first_product(c, w2_c, w2_s, eg_w, eg_s, E_ROW, True)
+            first_product(c, w1_c, w1_s, xg_w, xg_s, X_ROW, False)
 
         two = tile("two", [P, S * PACK], F32)
         tot = tile("tot", [P, V * PACK], F32)
         half_tanh = tile("half_tanh", [P, V * PACK], F32)
-        dev = tile("dev", [P, V * PACK], F32)
+        scaled = tile("scaled", [P, V * PACK], F32)
+        offset = tile("offset", [P, V * PACK], F32)
+        unit8 = tile("unit8", [P, PACK], F32)
         coef = tile("coef", [P, V * PACK], F32)
         unit4 = tile("unit4", [P, PACK], F32)
         hid = [tile("hid%d" % c, [P, CH * PACK], BF16) for c in range(NCH)]
         hid_c = [tile("hid_c%d" % c, [P, CH], U32) for c in range(NCH)]
         hid_s = [tile("hid_s%d" % c, [P, CH], U8) for c in range(NCH)]
         res = [tile("res%d" % c, [P, 2 * CH], F32) for c in range(NCH)]
-        acc = [ps.tile([P, 2 * CH], F32, name="acc%d" % c) for c in range(NCH)]
         VH = V // 2
 
         def do_tanh(c):
@@ -178,25 +184,29 @@ def tile_picked_yprimr_step_p_kernel(
                 tot[:, vslice(h)].rearrange("p (v t) -> p v t", t=PACK), g[:, :, 0, :], g[:, :, 2, :], ALU.add
             )
 
-        def do_sig(h):
-            nc.scalar.activation(half_tanh[:, vslice(h)], tot[:, vslice(h)], ACT.Tanh, scale=0.4)
+        def by_t(x, h):
+            return x[:, vslice(h)].rearrange("p (t v) -> p v t", t=PACK)
 
-        def do_dev(h):
-            nc.vector.scalar_tensor_tensor(
-                dev[:, vslice(h)].rearrange("p (v t) -> p v t", t=PACK),
-                lab_t[:].rearrange("p (t v) -> p v t", t=PACK)[:, h * VH : (h + 1) * VH, :],
-                -2.0,
-                half_tanh[:, vslice(h)].rearrange("p (v t) -> p v t", t=PACK),
-                ALU.mult, ALU.add,
+        def do_sig(h):
+            nc.scalar.activation(
+                by_t(half_tanh, h), tot[:, vslice(h)].rearrange("p (v t) -> p v t", t=PACK), ACT.Tanh, scale=0.4
+            )
+            for t in range(PACK):
+                run = slice((h * PACK + t) * VH, (h * PACK + t + 1) * VH)
+                nc.scalar.activation(scaled[:, run], half_tanh[:, run], ACT.Copy, scale=unit4[:, t : t + 1])
+
+        def do_offset(t):
+            nc.vector.tensor_scalar(
+                offset[:, t * V : (t + 1) * V], lab_t[:, t * V : (t + 1) * V],
+                unit8[:, t : t + 1], unit4[:, t : t + 1], ALU.mult, ALU.add,
             )
 
         def do_coef(h):
-            nc.vector.scalar_tensor_tensor(
+            nc.vector.tensor_tensor(
                 coef[:, vslice(h)].rearrange("p (v t) -> p v t", t=PACK),
-                dev[:, vslice(h)].rearrange("p (v t) -> p v t", t=PACK),
-                1.0,
-                unit4[:].unsqueeze(1).to_broadcast([P, VH, PACK]),
-                ALU.add, ALU.mult,
+                by_t(scaled, h),
+                offset[:].rearrange("p (t v) -> p v t", t=PACK)[:, h * VH : (h + 1) * VH, :],
+                ALU.add,
             )
 
         def do_hid(c):
@@ -217,41 +227,43 @@ def tile_picked_yprimr_step_p_kernel(
         def do_out(c):
             for a in range(2):
                 m = slice(a * P, (a + 1) * P)
+                acc = ps.tile([P, CH], F32, name="acc%d_%d" % (c, a), tag="bank%d" % (2 * c + a))
                 nc.tensor.matmul_mx(
-                    out=acc[c][:, a * CH : (a + 1) * CH],
+                    out=acc[:],
                     lhsT=w3_c[:, m].bitcast(FP8X4), lhsT_scale=w3_s[:, m],
                     rhs=hid_c[c][:].bitcast(FP8X4), rhs_scale=hid_s[c][:],
                     start=True, stop=True,
                 )
-            nc.scalar.copy(res[c][:], acc[c][:])
+                nc.scalar.copy(res[c][:, a * CH : (a + 1) * CH], acc[:])
             nc.sync.dma_start(
                 out=out[:, c * CH : (c + 1) * CH].rearrange("(a p) j -> p a j", a=2),
                 in_=res[c][:].rearrange("p (a j) -> p a j", a=2),
             )
 
         nc.scalar.activation(unit4[:], unit_t[:], ACT.Copy, scale=0.4)
+        nc.scalar.activation(unit8[:], unit_t[:], ACT.Copy, scale=-0.8)
+        for t in range(PACK):
+            do_offset(t)
         do_tanh(0)
         do_tanh(1)
         do_two(0)
         do_tanh(2)
         do_two(1)
         do_tanh(3)
-        do_two(2)
         do_tot(0)
         do_sig(0)
+        do_two(2)
         do_two(3)
-        do_dev(0)
-        do_tot(1)
-        do_sig(1)
         nc.scalar.copy(
             w3_bf[:].rearrange("p (c i j) -> p c j i", i=4, j=PACK),
             w3_raw[:].rearrange("p (j c i) -> p c j i", i=4, j=PACK),
         )
         do_coef(0)
-        do_dev(1)
+        do_tot(1)
+        do_sig(1)
         do_hid(0)
-        do_coef(1)
         do_hid(1)
+        do_coef(1)
         nc.vector.quantize_mx(out=w3_c[:].bitcast(FP8X4), scales=w3_s[:], in_=w3_bf[:])
         do_quant(0)
         do_hid(2)

@@ -9,8 +9,8 @@ PACK = 4
 CH = 128
 NCH = S // CH
 HALF = S // 2
-SPLIT1 = 44
-SPLIT2 = 44
+SPLIT = 88
+FILL = 48
 X_ROW = 4
 E_ROW = 8
 FLOPS = 2 * (2 * K * H * S + H * N * S)
@@ -35,7 +35,7 @@ def tile_picked_yprimr_step_p_kernel(
         ps = ctx.enter_context(tc.psum_pool(name="ps", bufs=1))
 
         def tile(name, shape, dtype):
-            return sb.tile(shape, dtype, name=name, align_bytes=64)
+            return sb.tile(shape, dtype, name=name, tag=name, align_bytes=64)
 
         offs_t = tile("offs_t", [P, S // 16], U16)
         rstp_t = tile("rstp_t", [P, S // 16], U16)
@@ -69,17 +69,17 @@ def tile_picked_yprimr_step_p_kernel(
         def load_rows(dst, src):
             nc.sync.dma_start(out=dst[:], in_=src.rearrange("(p j) c -> p (j c)", j=PACK))
 
+        nc.sync.dma_start(offs_t[:], offs)
         load_rows(w1_raw, w1)
+        nc.sync.dma_start(rstp_t[:], rstp)
+        load_rows(unit_t, unit)
         for r in range(4):
             load_scale_rows(nc.sync, xs, x_scales, r, X_ROW)
-        nc.sync.dma_start(offs_t[:], offs)
         load_rows(w2_raw, w2)
         for r in range(4):
             load_scale_rows(nc.sync, es, e_scales, r, E_ROW)
-        nc.sync.dma_start(rstp_t[:], rstp)
         load_words(xw, x_words)
         load_words(ew, e_words)
-        load_rows(unit_t, unit)
         load_rows(lab_t, lab)
         load_rows(w3_raw, w3)
 
@@ -91,7 +91,6 @@ def tile_picked_yprimr_step_p_kernel(
         w2_bf = tile("w2_bf", [P, H * PACK], BF16)
         w3_bf = tile("w3_bf", [P, N * PACK], BF16)
         w1_c = tile("w1_c", [P, H], U32)
-        w2_c = tile("w2_c", [P, H], U32)
         w3_c = tile("w3_c", [P, N], U32)
         w1_s = tile("w1_s", [P, H], U8)
         w2_s = tile("w2_s", [P, H], U8)
@@ -103,17 +102,15 @@ def tile_picked_yprimr_step_p_kernel(
         def dealt_out(bf):
             return bf[:].rearrange("p (t m j) -> p m j t", t=PACK, j=PACK)
 
-        def round_and_deal(bf, raw, sign, split):
-            nc.scalar.activation(dealt_out(bf)[:, :split], dealt_in(raw)[:, :split], ACT.Copy, scale=sign)
-            nc.vector.tensor_scalar(
-                dealt_out(bf)[:, split:], dealt_in(raw)[:, split:], sign, None, ALU.mult
-            )
-
-        round_and_deal(w1_bf, w1_raw, 1.0, SPLIT1)
+        nc.scalar.copy(dealt_out(w1_bf), dealt_in(w1_raw))
         nc.vector.tensor_copy(xg_s[:], xs[:].indirect(offs_t[:]))
         nc.vector.quantize_mx(out=w1_c[:].bitcast(FP8X4), scales=w1_s[:], in_=w1_bf[:])
-        round_and_deal(w2_bf, w2_raw, -1.0, SPLIT2)
+        nc.scalar.activation(dealt_out(w2_bf)[:, :SPLIT], dealt_in(w2_raw)[:, :SPLIT], ACT.Copy, scale=-1.0)
+        nc.vector.tensor_scalar(
+            dealt_out(w2_bf)[:, SPLIT:], dealt_in(w2_raw)[:, SPLIT:], -1.0, None, ALU.mult
+        )
         nc.vector.tensor_copy(eg_s[:], es[:].indirect(rstp_t[:]))
+        w2_c = sb.tile([P, H], U32, name="w2_c", tag="es", align_bytes=64)
         nc.vector.quantize_mx(out=w2_c[:].bitcast(FP8X4), scales=w2_s[:], in_=w2_bf[:])
 
         def gather_words(picked, window, places):
@@ -137,12 +134,12 @@ def tile_picked_yprimr_step_p_kernel(
                 )
 
         gather_words(xg_w, xw, offs_t)
-        for c in range(2):
+        for c in range(NCH - 1):
             first_product(c, w1_c, w1_s, xg_w, xg_s, X_ROW, True)
         gather_words(eg_w, ew, rstp_t)
-        for c in range(2):
+        for c in range(NCH - 1):
             first_product(c, w2_c, w2_s, eg_w, eg_s, E_ROW, False)
-        for c in range(2, NCH):
+        for c in range(NCH - 1, NCH):
             first_product(c, w2_c, w2_s, eg_w, eg_s, E_ROW, True)
             first_product(c, w1_c, w1_s, xg_w, xg_s, X_ROW, False)
 
@@ -167,9 +164,9 @@ def tile_picked_yprimr_step_p_kernel(
                 ACT.Tanh,
             )
 
-        def do_two(c):
-            lo = max(c * CH - 1, 0)
-            hi = S if c == NCH - 1 else (c + 1) * CH - 1
+        def do_two(j0, j1):
+            lo = max(j0 - 1, 0)
+            hi = S if j1 == S else j1 - 1
             nc.vector.tensor_tensor(
                 two[:, lo * PACK : hi * PACK], th[:, lo * PACK : hi * PACK],
                 th[:, (lo + 1) * PACK : (hi + 1) * PACK], ALU.add,
@@ -234,7 +231,10 @@ def tile_picked_yprimr_step_p_kernel(
                     rhs=hid_c[c][:].bitcast(FP8X4), rhs_scale=hid_s[c][:],
                     start=True, stop=True,
                 )
-                nc.scalar.copy(res[c][:, a * CH : (a + 1) * CH], acc[:])
+                if c == NCH - 1 and a == 1:
+                    nc.vector.tensor_copy(res[c][:, a * CH : (a + 1) * CH], acc[:])
+                else:
+                    nc.scalar.copy(res[c][:, a * CH : (a + 1) * CH], acc[:])
             nc.sync.dma_start(
                 out=out[:, c * CH : (c + 1) * CH].rearrange("(a p) j -> p a j", a=2),
                 in_=res[c][:].rearrange("p (a j) -> p a j", a=2),
@@ -246,14 +246,15 @@ def tile_picked_yprimr_step_p_kernel(
             do_offset(t)
         do_tanh(0)
         do_tanh(1)
-        do_two(0)
+        do_two(0, CH)
         do_tanh(2)
-        do_two(1)
+        do_two(CH, 2 * CH)
+        do_two(2 * CH, 2 * CH + FILL)
         do_tanh(3)
         do_tot(0)
         do_sig(0)
-        do_two(2)
-        do_two(3)
+        do_two(2 * CH + FILL, 3 * CH)
+        do_two(3 * CH, 4 * CH)
         nc.scalar.copy(
             w3_bf[:].rearrange("p (c i j) -> p c j i", i=4, j=PACK),
             w3_raw[:].rearrange("p (j c i) -> p c j i", i=4, j=PACK),

from contextlib import ExitStack

import concourse.mybir as mybir

K, T, S, D, N, H = 512, 2048, 512, 4, 256, 512
V = S // D
P = 128
PACK = 4
CH = 128
NCH = S // CH
HALF = S // 2
SPLIT = 88
FILL = 48
X_ROW = 4
E_ROW = 8
FLOPS = 2 * (2 * K * H * S + H * N * S)

F32 = mybir.dt.float32
BF16 = mybir.dt.bfloat16
I32 = mybir.dt.int32
U32 = mybir.dt.uint32
U16 = mybir.dt.uint16
U8 = mybir.dt.uint8
FP8X4 = mybir.dt.float8_e4m3fn_x4
ALU = mybir.AluOpType
ACT = mybir.ActivationFunctionType


def tile_picked_yprimr_step_p_kernel(
    tc, x_words, x_scales, w1, e_words, e_scales, w2, lab, unit, w3, offs, rstp, out
):
    nc = tc.nc
    with ExitStack() as ctx:
        sb = ctx.enter_context(tc.tile_pool(name="sb", bufs=1))
        ps = ctx.enter_context(tc.psum_pool(name="ps", bufs=1))

        def tile(name, shape, dtype):
            return sb.tile(shape, dtype, name=name, tag=name, align_bytes=64)

        offs_t = tile("offs_t", [P, S // 16], U16)
        rstp_t = tile("rstp_t", [P, S // 16], U16)
        xw = tile("xw", [P, T], U32)
        ew = tile("ew", [P, T], U32)
        xs = tile("xs", [P, T], U8)
        es = tile("es", [P, T], U8)
        w1_raw = tile("w1_raw", [P, PACK * H], F32)
        w2_raw = tile("w2_raw", [P, PACK * H], F32)
        w3_raw = tile("w3_raw", [P, PACK * N], F32)
        lab_t = tile("lab_t", [P, PACK * V], F32)
        unit_t = tile("unit_t", [P, PACK], F32)
        th = tile("th", [P, (S + 1) * PACK], F32)

        nc.vector.memset(xs[:].bitcast(U32), 0)
        nc.vector.memset(es[:].bitcast(U32), 0)
        nc.vector.memset(th[:, S * PACK :], 0.0)

        def load_scale_rows(queue, plane, rows, r, first):
            queue.dma_start(
                out=plane[first + r : P : 32, :].bitcast(I32),
                in_=rows[0, r:16:4, :].bitcast(I32),
            )

        def load_words(window, words):
            nc.sync.dma_start(
                out=window[:].bitcast(I32),
                in_=words[0].rearrange("p n t -> p (n t)").bitcast(I32),
            )

        def load_rows(dst, src):
            nc.sync.dma_start(out=dst[:], in_=src.rearrange("(p j) c -> p (j c)", j=PACK))

        nc.sync.dma_start(offs_t[:], offs)
        load_rows(w1_raw, w1)
        nc.sync.dma_start(rstp_t[:], rstp)
        load_rows(unit_t, unit)
        for r in range(4):
            load_scale_rows(nc.sync, xs, x_scales, r, X_ROW)
        load_rows(w2_raw, w2)
        for r in range(4):
            load_scale_rows(nc.sync, es, e_scales, r, E_ROW)
        load_words(xw, x_words)
        load_words(ew, e_words)
        load_rows(lab_t, lab)
        load_rows(w3_raw, w3)

        xg_s = tile("xg_s", [P, S], U8)
        eg_s = tile("eg_s", [P, S], U8)
        xg_w = [tile("xg_w%d" % h, [P, HALF], U32) for h in range(2)]
        eg_w = [tile("eg_w%d" % h, [P, HALF], U32) for h in range(2)]
        w1_bf = tile("w1_bf", [P, H * PACK], BF16)
        w2_bf = tile("w2_bf", [P, H * PACK], BF16)
        w3_bf = tile("w3_bf", [P, N * PACK], BF16)
        w1_c = tile("w1_c", [P, H], U32)
        w3_c = tile("w3_c", [P, N], U32)
        w1_s = tile("w1_s", [P, H], U8)
        w2_s = tile("w2_s", [P, H], U8)
        w3_s = tile("w3_s", [P, N], U8)

        def dealt_in(raw):
            return raw[:].rearrange("p (j m t) -> p m j t", j=PACK, t=PACK)

        def dealt_out(bf):
            return bf[:].rearrange("p (t m j) -> p m j t", t=PACK, j=PACK)

        nc.scalar.copy(dealt_out(w1_bf), dealt_in(w1_raw))
        nc.vector.tensor_copy(xg_s[:], xs[:].indirect(offs_t[:]))
        nc.vector.quantize_mx(out=w1_c[:].bitcast(FP8X4), scales=w1_s[:], in_=w1_bf[:])
        nc.scalar.activation(dealt_out(w2_bf)[:, :SPLIT], dealt_in(w2_raw)[:, :SPLIT], ACT.Copy, scale=-1.0)
        nc.vector.tensor_scalar(
            dealt_out(w2_bf)[:, SPLIT:], dealt_in(w2_raw)[:, SPLIT:], -1.0, None, ALU.mult
        )
        nc.vector.tensor_copy(eg_s[:], es[:].indirect(rstp_t[:]))
        w2_c = sb.tile([P, H], U32, name="w2_c", tag="es", align_bytes=64)
        nc.vector.quantize_mx(out=w2_c[:].bitcast(FP8X4), scales=w2_s[:], in_=w2_bf[:])

        def gather_words(picked, window, places):
            for h in range(2):
                nc.vector.tensor_copy(
                    picked[h][:], window[:].indirect(places[:, h * HALF // 16 : (h + 1) * HALF // 16])
                )

        diff = [ps.tile([P, PACK * CH], F32, name="diff%d" % c, tag="bank%d" % c) for c in range(NCH)]

        def first_product(c, w_c, w_s, picked, picked_s, row, opens):
            cols = slice(c * CH, (c + 1) * CH)
            local = slice((c % 2) * CH, (c % 2 + 1) * CH)
            for t in range(PACK):
                m = slice(t * P, (t + 1) * P)
                nc.tensor.matmul_mx(
                    out=diff[c][:, t * CH : (t + 1) * CH],
                    lhsT=w_c[:, m].bitcast(FP8X4), lhsT_scale=w_s[:, m],
                    rhs=picked[c // 2][:, local].bitcast(FP8X4), rhs_scale=picked_s[row:, cols],
                    start=(opens and t == 0), stop=(not opens and t == PACK - 1),
                )

        gather_words(xg_w, xw, offs_t)
        for c in range(NCH - 1):
            first_product(c, w1_c, w1_s, xg_w, xg_s, X_ROW, True)
        gather_words(eg_w, ew, rstp_t)
        for c in range(NCH - 1):
            first_product(c, w2_c, w2_s, eg_w, eg_s, E_ROW, False)
        for c in range(NCH - 1, NCH):
            first_product(c, w2_c, w2_s, eg_w, eg_s, E_ROW, True)
            first_product(c, w1_c, w1_s, xg_w, xg_s, X_ROW, False)

        two = tile("two", [P, S * PACK], F32)
        tot = tile("tot", [P, V * PACK], F32)
        half_tanh = tile("half_tanh", [P, V * PACK], F32)
        scaled = tile("scaled", [P, V * PACK], F32)
        offset = tile("offset", [P, V * PACK], F32)
        unit8 = tile("unit8", [P, PACK], F32)
        coef = tile("coef", [P, V * PACK], F32)
        unit4 = tile("unit4", [P, PACK], F32)
        hid = [tile("hid%d" % c, [P, CH * PACK], BF16) for c in range(NCH)]
        hid_c = [tile("hid_c%d" % c, [P, CH], U32) for c in range(NCH)]
        hid_s = [tile("hid_s%d" % c, [P, CH], U8) for c in range(NCH)]
        res = [tile("res%d" % c, [P, 2 * CH], F32) for c in range(NCH)]
        VH = V // 2

        def do_tanh(c):
            nc.scalar.activation(
                th[:, c * CH * PACK : (c + 1) * CH * PACK].rearrange("p (j t) -> p j t", t=PACK),
                diff[c][:].rearrange("p (t j) -> p j t", t=PACK),
                ACT.Tanh,
            )

        def do_two(j0, j1):
            lo = max(j0 - 1, 0)
            hi = S if j1 == S else j1 - 1
            nc.vector.tensor_tensor(
                two[:, lo * PACK : hi * PACK], th[:, lo * PACK : hi * PACK],
                th[:, (lo + 1) * PACK : (hi + 1) * PACK], ALU.add,
            )

        def vslice(h):
            return slice(h * VH * PACK, (h + 1) * VH * PACK)

        def do_tot(h):
            g = two[:, h * HALF * PACK : (h + 1) * HALF * PACK].rearrange("p (v d t) -> p v d t", d=D, t=PACK)
            nc.vector.tensor_tensor(
                tot[:, vslice(h)].rearrange("p (v t) -> p v t", t=PACK), g[:, :, 0, :], g[:, :, 2, :], ALU.add
            )

        def by_t(x, h):
            return x[:, vslice(h)].rearrange("p (t v) -> p v t", t=PACK)

        def do_sig(h):
            nc.scalar.activation(
                by_t(half_tanh, h), tot[:, vslice(h)].rearrange("p (v t) -> p v t", t=PACK), ACT.Tanh, scale=0.4
            )
            for t in range(PACK):
                run = slice((h * PACK + t) * VH, (h * PACK + t + 1) * VH)
                nc.scalar.activation(scaled[:, run], half_tanh[:, run], ACT.Copy, scale=unit4[:, t : t + 1])

        def do_offset(t):
            nc.vector.tensor_scalar(
                offset[:, t * V : (t + 1) * V], lab_t[:, t * V : (t + 1) * V],
                unit8[:, t : t + 1], unit4[:, t : t + 1], ALU.mult, ALU.add,
            )

        def do_coef(h):
            nc.vector.tensor_tensor(
                coef[:, vslice(h)].rearrange("p (v t) -> p v t", t=PACK),
                by_t(scaled, h),
                offset[:].rearrange("p (t v) -> p v t", t=PACK)[:, h * VH : (h + 1) * VH, :],
                ALU.add,
            )

        def do_hid(c):
            vc = CH // D
            nc.vector.tensor_tensor(
                hid[c][:].rearrange("p (v d t) -> p v d t", d=D, t=PACK),
                two[:, c * CH * PACK : (c + 1) * CH * PACK].rearrange("p (v d t) -> p v d t", d=D, t=PACK),
                coef[:, c * vc * PACK : (c + 1) * vc * PACK]
                .rearrange("p (v t) -> p v t", t=PACK)
                .unsqueeze(2)
                .to_broadcast([P, vc, D, PACK]),
                ALU.mult,
            )

        def do_quant(c):
            nc.vector.quantize_mx(out=hid_c[c][:].bitcast(FP8X4), scales=hid_s[c][:], in_=hid[c][:])

        def do_out(c):
            for a in range(2):
                m = slice(a * P, (a + 1) * P)
                acc = ps.tile([P, CH], F32, name="acc%d_%d" % (c, a), tag="bank%d" % (2 * c + a))
                nc.tensor.matmul_mx(
                    out=acc[:],
                    lhsT=w3_c[:, m].bitcast(FP8X4), lhsT_scale=w3_s[:, m],
                    rhs=hid_c[c][:].bitcast(FP8X4), rhs_scale=hid_s[c][:],
                    start=True, stop=True,
                )
                if c == NCH - 1 and a == 1:
                    nc.vector.tensor_copy(res[c][:, a * CH : (a + 1) * CH], acc[:])
                else:
                    nc.scalar.copy(res[c][:, a * CH : (a + 1) * CH], acc[:])
            nc.sync.dma_start(
                out=out[:, c * CH : (c + 1) * CH].rearrange("(a p) j -> p a j", a=2),
                in_=res[c][:].rearrange("p (a j) -> p a j", a=2),
            )

        nc.scalar.activation(unit4[:], unit_t[:], ACT.Copy, scale=0.4)
        nc.scalar.activation(unit8[:], unit_t[:], ACT.Copy, scale=-0.8)
        for t in range(PACK):
            do_offset(t)
        do_tanh(0)
        do_tanh(1)
        do_two(0, CH)
        do_tanh(2)
        do_two(CH, 2 * CH)
        do_two(2 * CH, 2 * CH + FILL)
        do_tanh(3)
        do_tot(0)
        do_sig(0)
        do_two(2 * CH + FILL, 3 * CH)
        do_two(3 * CH, 4 * CH)
        nc.scalar.copy(
            w3_bf[:].rearrange("p (c i j) -> p c j i", i=4, j=PACK),
            w3_raw[:].rearrange("p (j c i) -> p c j i", i=4, j=PACK),
        )
        do_coef(0)
        do_tot(1)
        do_sig(1)
        do_hid(0)
        do_hid(1)
        do_coef(1)
        nc.vector.quantize_mx(out=w3_c[:].bitcast(FP8X4), scales=w3_s[:], in_=w3_bf[:])
        do_quant(0)
        do_hid(2)
        do_out(0)
        do_quant(1)
        do_hid(3)
        do_out(1)
        do_quant(2)
        do_quant(3)
        do_out(2)
        do_out(3)
